import numpy as np
import ml_dtypes


def mxq(x, axis, fmt="e4m3"):
    dtype, down = {"e4m3": (ml_dtypes.float8_e4m3fn, 7), "e5m2": (ml_dtypes.float8_e5m2, 14)}[fmt]
    v = np.moveaxis(np.asarray(x, np.float32).astype(ml_dtypes.bfloat16).astype(np.float64), axis, -1)
    blocks = v.reshape(v.shape[:-1] + (-1, 32))
    amax = np.abs(blocks).max(-1, keepdims=True)
    byte = np.maximum(np.where(amax > 0, np.frexp(amax)[1] - 1 + 127, 0) - down, 1)
    scale = np.exp2(byte - 127.0)
    codes = (blocks / scale).astype(np.float32).astype(dtype).astype(np.float64)
    return np.moveaxis((codes * scale).reshape(v.shape), -1, axis)


WIDE = False


def mx_kscale(k):
    if not WIDE:
        return np.ones(k)
    levels = np.array([10, -10, 5, -5, 0])
    if k % 512:
        return np.exp2(np.random.permutation(np.resize(levels, k // 32))).repeat(32)
    a = np.empty((k // 512, 16))
    for p in range(k // 512):
        a[p, :8] = np.random.permutation(np.resize(levels, 8))
        for g in range(8):
            far = levels[np.abs(levels - a[p, g]) >= 10]
            a[p, g + 8] = far[np.random.randint(len(far))]
    return np.exp2(a.ravel()).repeat(32)


def f64(x):
    return np.asarray(x).astype(np.float64)


def striped(idx):
    return np.tile(idx.reshape(-1, 16).T, (8, 1)).astype(np.uint16)


def unstriped(offs):
    return offs[:16].T.reshape(-1).astype(np.int64)


def striped8(idx):
    return np.concatenate([x.reshape(-1, 16).T for x in idx]).astype(np.uint16)


def runs(offs, k):
    lists = np.stack([offs[16 * r : 16 * r + 16].T.reshape(-1) for r in range(8)]).astype(np.int64)
    return lists[np.arange(k) % 512 // 64]


def pack_weight(w):
    k, n = w.shape
    w = f64(np.asarray(w, np.float32).astype(ml_dtypes.bfloat16)).reshape(k // 32, 32, n)
    amax = np.abs(w).max(1)
    byte = np.clip(np.where(amax > 0, np.frexp(amax)[1] - 1 + 127 - 7, 1), 1, 254)
    scaled = (w * np.exp2(127.0 - byte)[:, None, :]).reshape(k, n).astype(np.float32)
    words = np.ascontiguousarray(scaled.reshape(k // 512, 128, 4, n).transpose(0, 1, 3, 2)).astype(ml_dtypes.float8_e4m3fn).view(np.uint8)
    return words, np.ascontiguousarray(byte.astype(np.uint8).reshape(k // 512, 16, n))


def unpack_weight(words, scales):
    g, p, n, _ = words.shape
    vals = np.ascontiguousarray(words).view(ml_dtypes.float8_e4m3fn).astype(np.float64) * np.repeat(np.exp2(scales.astype(np.float64) - 127.0), 8, axis=1)[..., None]
    return vals.transpose(0, 1, 3, 2).reshape(g * 512, n)


def relu(v):
    return np.maximum(v, 0.0)


def sigmoid(v):
    return 1.0 / (1.0 + np.exp(-np.maximum(v, -700.0)))


K, T, S, N, H, W = 512, 2048, 512, 512, 512, 256


def setup_inputs():
    n = np.random.standard_normal
    s = mx_kscale(K)[:, None]
    u = mx_kscale(S)
    packed_xT = pack_weight(n((K, T)) * s)
    perm = np.stack([np.random.permutation(H) for _ in range(8)])
    return {
        "x_words": packed_xT[0],
        "x_scales": packed_xT[1],
        "wa": (n((K, H)) / np.sqrt(K) / s).astype(np.float32),
        "wb": (n((K, N)) / np.sqrt(K) / s).astype(np.float32),
        "gt": (np.random.uniform(0.5, 1.5, (S, 1)) * u[:, None]).astype(np.float32),
        "gi": (np.random.uniform(0.5, 1.5, (S, 1)) / u[:, None]).astype(np.float32),
        "offs": striped(np.random.permutation(T)[:S]),
        "two": striped(np.random.permutation(T)[:S]),
        "n1": striped8(perm[:, :W]),
        "n2": striped8(perm[:, W:]),
        "n3": striped8(np.stack([np.random.permutation(N) for _ in range(8)])),
        "n4": striped8(np.stack([np.random.permutation(N) for _ in range(8)])),
        "n5": striped8(np.stack([np.random.permutation(N) for _ in range(8)])),
    }


def reference(x_words, x_scales, wa, wb, gt, gi, offs, two, n1, n2, n3, n4, n5):
    xq = unpack_weight(x_words, x_scales)[:, unstriped(offs)]
    a = xq.T @ mxq(f64(wa), 0, "e4m3")
    pa = a[np.arange(S)[:, None], runs(n1, S)]
    pb = a[np.arange(S)[:, None], runs(n2, S)]
    ra = pa * sigmoid(pb)
    ds = a.copy()
    ds[np.arange(S)[:, None], runs(n2, S)] = ra
    z = f64(gt) * ds
    x_two = unpack_weight(x_words, x_scales)[:, unstriped(two)]
    b = x_two.T @ mxq(f64(wb), 0, "e4m3")
    z2 = f64(gi) * (relu(b - (b[np.arange(S)[:, None], runs(n3, S)])) + 0.5 * (relu(b[np.arange(S)[:, None], runs(n4, S)] - b)))
    cv = 0.0625 * ((mxq(z, 0, "e4m3").T @ mxq(z2, 0, "e4m3")))
    rl = relu(cv)
    ds2 = np.zeros((H, N))
    ds2[np.arange(H)[:, None], runs(n5, H)] = rl
    return ds2 - (0.5 * cv)

@@ -1,0 +1,288 @@
+from contextlib import ExitStack
+
+import concourse.mybir as mybir
+from concourse.masks import make_identity
+
+K, T, S, H, N, W = 512, 2048, 512, 512, 512, 256
+FLOPS = 3 * 2 * 512 * 512 * 512
+
+F32 = mybir.dt.float32
+BF16 = mybir.dt.bfloat16
+I32 = mybir.dt.int32
+U32 = mybir.dt.uint32
+U16 = mybir.dt.uint16
+U8 = mybir.dt.uint8
+FP8X4 = mybir.dt.float8_e4m3fn_x4
+ALU = mybir.AluOpType
+ACT = mybir.ActivationFunctionType
+
+P = 128
+PACK = 4
+
+
+def tile_picked_mombfoldhingesend_none_p_kernel(
+    tc, x_words, x_scales, wa, wb, gt, gi, offs, two, n1, n2, n3, n4, n5, out
+):
+    nc = tc.nc
+    with ExitStack() as ctx:
+        keep = ctx.enter_context(tc.tile_pool(name="keep", bufs=1))
+        psum = ctx.enter_context(tc.psum_pool(name="psum", bufs=7))
+        psum_turn = ctx.enter_context(tc.psum_pool(name="psum_turn", bufs=1))
+
+        def sb(name, shape, dtype):
+            return keep.tile(shape, dtype, name=name, align_bytes=64)
+
+        def load_list(name, src):
+            tile = sb(name, list(src.shape), U16)
+            nc.sync.dma_start(tile[:], src)
+            return tile
+
+        def weave(engine_copy, dst, src):
+            engine_copy(
+                dst.rearrange("p (c i t) -> p c t i", i=4, t=PACK),
+                src.rearrange("p t (c i) -> p c t i", i=4),
+            )
+
+        warm = sb("warm", [P, 2], F32)
+        scale_table = sb("scale_table", [P, T], U8)
+        nc.vector.memset(scale_table[:, :1280].bitcast(I32), 0)
+        nc.gpsimd.memset(scale_table[:, 1280:].bitcast(I32), 0)
+        nc.gpsimd.memset(warm[:, 0:1], 0.0)
+        nc.scalar.activation(warm[:, 1:2], warm[:, 0:1], ACT.Sigmoid)
+
+        two_t = load_list("two_t", two)
+        offs_t = load_list("offs_t", offs)
+        for q in range(4):
+            nc.sync.dma_start(
+                scale_table[32 * q : 32 * q + 4, :].bitcast(I32),
+                x_scales[0, 4 * q : 4 * q + 4, :].bitcast(I32),
+            )
+        word_table = sb("word_table", [P, T], I32)
+        nc.sync.dma_start(word_table[:], x_words[0].rearrange("p c r -> p (c r)").bitcast(I32))
+        wb_rows = wb.rearrange("(p j) n -> p j n", j=PACK)
+        wb_raw = []
+        for h in range(2):
+            raw = sb("wb_raw%d" % h, [P, PACK, N // 2], F32)
+            nc.sync.dma_start(raw[:], wb_rows[:, :, h * 256 : (h + 1) * 256])
+            wb_raw.append(raw)
+        gi_t = sb("gi_t", [P, PACK], F32)
+        nc.sync.dma_start(gi_t[:], gi.rearrange("(p t) o -> p (t o)", t=PACK))
+        n3_t = load_list("n3_t", n3)
+        n4_t = load_list("n4_t", n4)
+        wa_raw = sb("wa_raw", [P, PACK, H], F32)
+        nc.sync.dma_start(wa_raw[:], wa.rearrange("(p j) n -> p j n", j=PACK))
+        gt_t = sb("gt_t", [P, PACK], F32)
+        nc.sync.dma_start(gt_t[:], gt.rearrange("(p t) o -> p (t o)", t=PACK))
+        n1_t = load_list("n1_t", n1)
+        n2_t = load_list("n2_t", n2)
+        n5_t = load_list("n5_t", n5)
+
+        b_win = [sb("b_win%d" % t, [P, 2 * N], F32) for t in range(PACK)]
+        for t in range(PACK):
+            nc.gpsimd.memset(b_win[t][:, N:], 0.0)
+
+        ident = sb("ident", [P, P], F32)
+        make_identity(nc, ident[:])
+
+        sgn = sb("sgn", [P, PACK], F32)
+        nc.gpsimd.tensor_scalar(sgn[:], gi_t[:], 0.0, -0.5, ALU.is_ge, ALU.add)
+        half_gi = sb("half_gi", [P, PACK], F32)
+        nc.gpsimd.tensor_tensor(half_gi[:], gi_t[:], sgn[:], ALU.mult)
+        gt2 = sb("gt2", [P, PACK], F32)
+        nc.gpsimd.tensor_scalar(gt2[:], gt_t[:], 2.0, 0.0, ALU.mult, ALU.add)
+        gts = sb("gts", [P, PACK], F32)
+        nc.gpsimd.tensor_tensor(gts[:], gt2[:], sgn[:], ALU.mult)
+
+        def pick_scales(name, lst):
+            plain = sb(name + "_plain", [P, S], U8)
+            nc.vector.tensor_copy(plain[:], scale_table[:].indirect(lst[:]))
+            dealt = sb(name + "_dealt", [P, S], U8)
+            nc.vector.tensor_copy(
+                dealt[:].rearrange("p (t m) -> p m t", t=PACK),
+                plain[:].rearrange("p (m t) -> p m t", t=PACK),
+            )
+            return dealt
+
+        def pick_words(name, lst):
+            dealt = sb(name, [P, S], U32)
+            nc.vector.tensor_copy(
+                dealt[:].rearrange("p (t m) -> p m t", t=PACK),
+                word_table[:].bitcast(U32).indirect(lst[:]),
+            )
+            return dealt
+
+        xb_scales = pick_scales("xb_scales", two_t)
+        xa_scales = pick_scales("xa_scales", offs_t)
+        xb_words = pick_words("xb_words", two_t)
+
+        wb_codes = sb("wb_codes", [P, N], U32)
+        wb_scales = sb("wb_scales", [P, N], U8)
+        wb_woven = [sb("wb_woven%d" % h, [P, PACK * 256], BF16) for h in range(2)]
+        for h in range(2):
+            weave(nc.scalar.copy, wb_woven[h][:], wb_raw[h][:])
+        for h in range(2):
+            cols = slice(h * 256, (h + 1) * 256)
+            nc.vector.quantize_mx(wb_codes[:, cols].bitcast(FP8X4), wb_scales[:, cols], wb_woven[h][:])
+        xa_words = pick_words("xa_words", offs_t)
+
+        b_acc = []
+        for t in range(PACK):
+            acc = psum.tile([P, N], F32, name="acc")
+            rows = slice(t * P, (t + 1) * P)
+            nc.tensor.matmul_mx(
+                acc[:], xb_words[:, rows].bitcast(FP8X4), xb_scales[:, rows],
+                wb_codes[:].bitcast(FP8X4), wb_scales[:], start=True, stop=True,
+            )
+            b_acc.append(acc)
+
+        wa_woven = sb("wa_woven", [P, PACK * H], BF16)
+        weave(nc.vector.tensor_copy, wa_woven[:], wa_raw[:])
+        wa_codes = sb("wa_codes", [P, H], U32)
+        wa_scales = sb("wa_scales", [P, H], U8)
+        nc.vector.quantize_mx(wa_codes[:].bitcast(FP8X4), wa_scales[:], wa_woven[:])
+        a_acc = []
+        for t in range(PACK):
+            acc = psum.tile([P, H], F32, name="acc")
+            rows = slice(t * P, (t + 1) * P)
+            nc.tensor.matmul_mx(
+                acc[:], xa_words[:, rows].bitcast(FP8X4), xa_scales[:, rows],
+                wa_codes[:].bitcast(FP8X4), wa_scales[:], start=True, stop=True,
+            )
+            a_acc.append(acc)
+
+        b_plain = [sb("b_plain%d" % t, [P, N], F32) for t in range(PACK)]
+        a_win = [sb("a_win%d" % t, [P, H], F32) for t in range(PACK)]
+        gate = [sb("gate%d" % t, [P, W], F32) for t in range(PACK)]
+        z2_planes = sb("z2_planes", [P, PACK, N], BF16)
+        z_planes = sb("z_planes", [P, PACK, H], BF16)
+
+        def b_out(t):
+            nc.scalar.activation(b_win[t][:, :N], b_acc[t][:], ACT.Copy, scale=half_gi[:, t : t + 1])
+            nc.scalar.activation(b_plain[t][:], b_acc[t][:], ACT.Copy, scale=half_gi[:, t : t + 1])
+
+        def b_hinge(t):
+            d3 = sb("d3_%d" % t, [P, N], F32)
+            nc.vector.tensor_tensor(d3[:], b_win[t][:].indirect(n3_t[:]), b_plain[t][:], ALU.subtract)
+            d4 = sb("d4_%d" % t, [P, N], F32)
+            nc.vector.tensor_tensor(d4[:], b_win[t][:].indirect(n4_t[:]), b_plain[t][:], ALU.subtract)
+            r3 = sb("r3_%d" % t, [P, N], F32)
+            nc.scalar.activation(r3[:], d3[:], ACT.Relu, scale=-2.0)
+            return d4, r3
+
+        def b_sum(t, d4, r3):
+            nc.vector.scalar_tensor_tensor(z2_planes[:, t, :], d4[:], 0.0, r3[:], ALU.max, ALU.add)
+
+        def a_out(t):
+            nc.scalar.copy(a_win[t][:], a_acc[t][:])
+            nc.scalar.activation(gate[t][:], a_win[t][:].indirect(n2_t[:]), ACT.Sigmoid)
+
+        def a_pick(t):
+            pa = sb("pa%d" % t, [P, W], F32)
+            nc.vector.tensor_copy(pa[:], a_win[t][:].indirect(n1_t[:]))
+            return pa
+
+        def a_fold(t, pa):
+            nc.vector.tensor_tensor(a_win[t][:].indirect(n2_t[:]), pa[:], gate[t][:], ALU.mult)
+
+        def a_round(t):
+            nc.scalar.activation(
+                z_planes[:, t, :].rearrange("p (u m) -> p m u", u=PACK),
+                a_win[t][:].rearrange("p (m u) -> p m u", u=PACK),
+                ACT.Copy, scale=gts[:, t : t + 1],
+            )
+
+        b_out(0)
+        b_out(1)
+        h0 = b_hinge(0)
+        b_out(2)
+        h1 = b_hinge(1)
+        b_sum(0, *h0)
+        b_out(3)
+        h2 = b_hinge(2)
+        b_sum(1, *h1)
+        a_out(0)
+        h3 = b_hinge(3)
+        b_sum(2, *h2)
+        a_out(1)
+        p0 = a_pick(0)
+        b_sum(3, *h3)
+        a_fold(0, p0)
+        a_out(2)
+        p1 = a_pick(1)
+        a_out(3)
+        p2 = a_pick(2)
+        a_fold(1, p1)
+        z2_woven = sb("z2_woven", [P, PACK * N], BF16)
+        weave(nc.scalar.copy, z2_woven[:], z2_planes[:])
+        a_round(0)
+        p3 = a_pick(3)
+        a_fold(2, p2)
+        a_round(1)
+        a_fold(3, p3)
+        a_round(2)
+        a_round(3)
+        z2_codes = sb("z2_codes", [P, N], U32)
+        z2_scales = sb("z2_scales", [P, N], U8)
+        nc.vector.quantize_mx(z2_codes[:].bitcast(FP8X4), z2_scales[:], z2_woven[:])
+
+        z_codes = [sb("z_codes%d" % u, [P, P], U32) for u in range(PACK)]
+        z_scales = [sb("z_scales%d" % u, [P, P], U8) for u in range(PACK)]
+        z_woven = [sb("z_woven%d" % u, [P, PACK * P], BF16) for u in range(PACK)]
+        out_rows = out.rearrange("(p u) n -> p u n", u=PACK)
+        sent = [sb("sent%d" % u, [P, 2 * N], F32) for u in range(PACK)]
+        less = [sb("less%d" % u, [P, N], F32) for u in range(PACK)]
+        rl = [sb("rl%d" % u, [P, N], F32) for u in range(PACK)]
+
+        def moment(u, engine_copy):
+            weave(engine_copy, z_woven[u][:], z_planes[:, :, u * P : (u + 1) * P])
+            nc.vector.quantize_mx(z_codes[u][:].bitcast(FP8X4), z_scales[u][:], z_woven[u][:])
+            acc = psum.tile([P, N], F32, name="acc")
+            nc.tensor.matmul_mx(
+                acc[:], z_codes[u][:].bitcast(FP8X4), z_scales[u][:],
+                z2_codes[:].bitcast(FP8X4), z2_scales[:], start=True, stop=True,
+            )
+            nc.scalar.activation(rl[u][:], acc[:], ACT.Relu, scale=0.0625)
+            return acc
+
+        def halve(u, acc):
+            nc.scalar.activation(less[u][:], acc[:], ACT.Copy, scale=-0.03125)
+
+        def send(u):
+            nc.vector.tensor_copy(sent[u][:].indirect(n5_t[:]), rl[u][:])
+
+        def finish_by_transposes(u):
+            turned = psum_turn.tile([P, N], F32, name="turn")
+            for c in range(PACK):
+                cols = slice(c * P, (c + 1) * P)
+                nc.tensor.matmul(turned[:, cols], less[u][:, cols], ident[:], start=True, stop=False, is_transpose=True)
+                nc.tensor.matmul(turned[:, cols], sent[u][:, cols], ident[:], start=False, stop=True, is_transpose=True)
+            turned_sb = sb("turned%d" % u, [P, N], F32)
+            nc.scalar.copy(turned_sb[:], turned[:])
+            back = psum_turn.tile([P, N], F32, name="turn")
+            for c in range(PACK):
+                cols = slice(c * P, (c + 1) * P)
+                nc.tensor.transpose(back[:, cols], turned_sb[:, cols], ident[:])
+            res = sb("res%d" % u, [P, N], F32)
+            nc.scalar.copy(res[:], back[:])
+            nc.sync.dma_start(out_rows[:, u, :], res[:])
+
+        acc0 = moment(0, nc.vector.tensor_copy)
+        acc1 = moment(1, nc.vector.tensor_copy)
+        acc2 = moment(2, nc.vector.tensor_copy)
+        send(0)
+        halve(0, acc0)
+        acc3 = moment(3, nc.scalar.copy)
+        halve(1, acc1)
+        send(1)
+        finish_by_transposes(0)
+        halve(2, acc2)
+        halve(3, acc3)
+        send(2)
+        finish_by_transposes(1)
+        send(3)
+        finish_by_transposes(2)
+        for h in range(2):
+            cols = slice(h * 256, (h + 1) * 256)
+            res = sb("res_last%d" % h, [P, 256], F32)
+            nc.vector.tensor_tensor(res[:], sent[3][:, cols], less[3][:, cols], ALU.add)
+            (nc.sync if h == 0 else nc.scalar).dma_start(out_rows[:, 3, cols], res[:])

@@ -26,11 +26,13 @@ def tile_picked_mombfoldhingesend_none_p_kernel(
     nc = tc.nc
     with ExitStack() as ctx:
         keep = ctx.enter_context(tc.tile_pool(name="keep", bufs=1))
-        psum = ctx.enter_context(tc.psum_pool(name="psum", bufs=7))
-        psum_turn = ctx.enter_context(tc.psum_pool(name="psum_turn", bufs=1))
+        psum = ctx.enter_context(tc.psum_pool(name="psum", bufs=1))
 
-        def sb(name, shape, dtype):
-            return keep.tile(shape, dtype, name=name, align_bytes=64)
+        def bank(n):
+            return psum.tile([P, N], F32, name="bank%d" % n)
+
+        def sb(name, shape, dtype, tag=None):
+            return keep.tile(shape, dtype, name=name, tag=tag or name, align_bytes=64)
 
         def load_list(name, src):
             tile = sb(name, list(src.shape), U16)
@@ -57,39 +59,46 @@ def tile_picked_mombfoldhingesend_none_p_kernel(
                 scale_table[32 * q : 32 * q + 4, :].bitcast(I32),
                 x_scales[0, 4 * q : 4 * q + 4, :].bitcast(I32),
             )
+        wb_raw = sb("wb_raw", [P, PACK, N], F32)
+        nc.sync.dma_start(wb_raw[:], wb.rearrange("(p j) n -> p j n", j=PACK))
         word_table = sb("word_table", [P, T], I32)
         nc.sync.dma_start(word_table[:], x_words[0].rearrange("p c r -> p (c r)").bitcast(I32))
-        wb_rows = wb.rearrange("(p j) n -> p j n", j=PACK)
-        wb_raw = []
-        for h in range(2):
-            raw = sb("wb_raw%d" % h, [P, PACK, N // 2], F32)
-            nc.sync.dma_start(raw[:], wb_rows[:, :, h * 256 : (h + 1) * 256])
-            wb_raw.append(raw)
-        gi_t = sb("gi_t", [P, PACK], F32)
-        nc.sync.dma_start(gi_t[:], gi.rearrange("(p t) o -> p (t o)", t=PACK))
-        n3_t = load_list("n3_t", n3)
-        n4_t = load_list("n4_t", n4)
+        gates = sb("gates", [P, P], F32)
+        nc.gpsimd.memset(gates[:], 0.0)
+        for row, src in ((0, gi), (PACK, gt)):
+            nc.sync.dma_start(
+                gates[row : row + PACK, :].rearrange("t (g q) -> t g q", q=4),
+                src.rearrange("(g t q) o -> t g (q o)", t=PACK, q=4),
+            )
         wa_raw = sb("wa_raw", [P, PACK, H], F32)
         nc.sync.dma_start(wa_raw[:], wa.rearrange("(p j) n -> p j n", j=PACK))
-        gt_t = sb("gt_t", [P, PACK], F32)
-        nc.sync.dma_start(gt_t[:], gt.rearrange("(p t) o -> p (t o)", t=PACK))
+        n3_t = load_list("n3_t", n3)
+        n4_t = load_list("n4_t", n4)
         n1_t = load_list("n1_t", n1)
         n2_t = load_list("n2_t", n2)
         n5_t = load_list("n5_t", n5)
+
+        ident = sb("ident", [P, P], F32)
+        make_identity(nc, ident[:])
+        gates_turned = bank(7)
+        nc.tensor.transpose(gates_turned[:, :P], gates[:], ident[:])
+        gates_t = sb("gates_t", [P, 2 * PACK], F32)
+        nc.scalar.copy(gates_t[:], gates_turned[:, : 2 * PACK])
+        gi_t = gates_t[:, :PACK]
+        gt_t = gates_t[:, PACK:]
 
         b_win = [sb("b_win%d" % t, [P, 2 * N], F32) for t in range(PACK)]
         for t in range(PACK):
             nc.gpsimd.memset(b_win[t][:, N:], 0.0)
 
-        ident = sb("ident", [P, P], F32)
-        make_identity(nc, ident[:])
-
         sgn = sb("sgn", [P, PACK], F32)
-        nc.gpsimd.tensor_scalar(sgn[:], gi_t[:], 0.0, -0.5, ALU.is_ge, ALU.add)
+        nc.gpsimd.tensor_scalar(sgn[:], gi_t, 0.0, -0.5, ALU.is_ge, ALU.add)
         half_gi = sb("half_gi", [P, PACK], F32)
-        nc.gpsimd.tensor_tensor(half_gi[:], gi_t[:], sgn[:], ALU.mult)
+        nc.gpsimd.tensor_tensor(half_gi[:], gi_t, sgn[:], ALU.mult)
+        minus_gi = sb("minus_gi", [P, PACK], F32)
+        nc.gpsimd.tensor_scalar(minus_gi[:], half_gi[:], -2.0, 0.0, ALU.mult, ALU.add)
         gt2 = sb("gt2", [P, PACK], F32)
-        nc.gpsimd.tensor_scalar(gt2[:], gt_t[:], 2.0, 0.0, ALU.mult, ALU.add)
+        nc.gpsimd.tensor_scalar(gt2[:], gt_t, 2.0, 0.0, ALU.mult, ALU.add)
         gts = sb("gts", [P, PACK], F32)
         nc.gpsimd.tensor_tensor(gts[:], gt2[:], sgn[:], ALU.mult)
 
@@ -98,36 +107,32 @@ def tile_picked_mombfoldhingesend_none_p_kernel(
             nc.vector.tensor_copy(plain[:], scale_table[:].indirect(lst[:]))
             dealt = sb(name + "_dealt", [P, S], U8)
             nc.vector.tensor_copy(
-                dealt[:].rearrange("p (t m) -> p m t", t=PACK),
-                plain[:].rearrange("p (m t) -> p m t", t=PACK),
+                dealt[:].bitcast(I32).rearrange("p (t g) -> p t g", t=PACK),
+                plain[:].bitcast(I32).rearrange("p (g t) -> p t g", t=PACK),
             )
             return dealt
 
-        def pick_words(name, lst):
-            dealt = sb(name, [P, S], U32)
+        def pick_words(name, lst, tag=None):
+            dealt = sb(name, [P, S], U32, tag)
             nc.vector.tensor_copy(
-                dealt[:].rearrange("p (t m) -> p m t", t=PACK),
+                dealt[:].rearrange("p (t g q) -> p g t q", t=PACK, q=4),
                 word_table[:].bitcast(U32).indirect(lst[:]),
             )
             return dealt
 
         xb_scales = pick_scales("xb_scales", two_t)
         xa_scales = pick_scales("xa_scales", offs_t)
-        xb_words = pick_words("xb_words", two_t)
-
         wb_codes = sb("wb_codes", [P, N], U32)
         wb_scales = sb("wb_scales", [P, N], U8)
-        wb_woven = [sb("wb_woven%d" % h, [P, PACK * 256], BF16) for h in range(2)]
-        for h in range(2):
-            weave(nc.scalar.copy, wb_woven[h][:], wb_raw[h][:])
-        for h in range(2):
-            cols = slice(h * 256, (h + 1) * 256)
-            nc.vector.quantize_mx(wb_codes[:, cols].bitcast(FP8X4), wb_scales[:, cols], wb_woven[h][:])
-        xa_words = pick_words("xa_words", offs_t)
+        wb_woven = sb("wb_woven", [P, PACK * N], BF16)
+        weave(nc.scalar.copy, wb_woven[:, :1024], wb_raw[:, :, :256])
+        weave(nc.vector.tensor_copy, wb_woven[:, 1024:], wb_raw[:, :, 256:])
+        nc.vector.quantize_mx(wb_codes[:].bitcast(FP8X4), wb_scales[:], wb_woven[:])
+        xb_words = pick_words("xb_words", two_t)
 
         b_acc = []
         for t in range(PACK):
-            acc = psum.tile([P, N], F32, name="acc")
+            acc = bank(t)
             rows = slice(t * P, (t + 1) * P)
             nc.tensor.matmul_mx(
                 acc[:], xb_words[:, rows].bitcast(FP8X4), xb_scales[:, rows],
@@ -135,42 +140,78 @@ def tile_picked_mombfoldhingesend_none_p_kernel(
             )
             b_acc.append(acc)
 
+        xa_words = pick_words("xa_words", offs_t)
         wa_woven = sb("wa_woven", [P, PACK * H], BF16)
         weave(nc.vector.tensor_copy, wa_woven[:], wa_raw[:])
         wa_codes = sb("wa_codes", [P, H], U32)
         wa_scales = sb("wa_scales", [P, H], U8)
         nc.vector.quantize_mx(wa_codes[:].bitcast(FP8X4), wa_scales[:], wa_woven[:])
-        a_acc = []
-        for t in range(PACK):
-            acc = psum.tile([P, H], F32, name="acc")
+
+        def a_product(t):
+            acc = bank(t)
             rows = slice(t * P, (t + 1) * P)
             nc.tensor.matmul_mx(
                 acc[:], xa_words[:, rows].bitcast(FP8X4), xa_scales[:, rows],
                 wa_codes[:].bitcast(FP8X4), wa_scales[:], start=True, stop=True,
             )
-            a_acc.append(acc)
+            return acc
 
         b_plain = [sb("b_plain%d" % t, [P, N], F32) for t in range(PACK)]
         a_win = [sb("a_win%d" % t, [P, H], F32) for t in range(PACK)]
         gate = [sb("gate%d" % t, [P, W], F32) for t in range(PACK)]
-        z2_planes = sb("z2_planes", [P, PACK, N], BF16)
         z_planes = sb("z_planes", [P, PACK, H], BF16)
 
         def b_out(t):
-            nc.scalar.activation(b_win[t][:, :N], b_acc[t][:], ACT.Copy, scale=half_gi[:, t : t + 1])
-            nc.scalar.activation(b_plain[t][:], b_acc[t][:], ACT.Copy, scale=half_gi[:, t : t + 1])
+            nc.scalar.copy(b_win[t][:, :N], b_acc[t][:])
+            if t < 2:
+                nc.scalar.copy(b_plain[t][:], b_acc[t][:])
+            else:
+                nc.sync.dma_start(b_plain[t][:], b_win[t][:, :N])
+
+        sum_bank = [bank(PACK + f) for f in range(PACK)]
 
         def b_hinge(t):
             d3 = sb("d3_%d" % t, [P, N], F32)
             nc.vector.tensor_tensor(d3[:], b_win[t][:].indirect(n3_t[:]), b_plain[t][:], ALU.subtract)
             d4 = sb("d4_%d" % t, [P, N], F32)
             nc.vector.tensor_tensor(d4[:], b_win[t][:].indirect(n4_t[:]), b_plain[t][:], ALU.subtract)
-            r3 = sb("r3_%d" % t, [P, N], F32)
-            nc.scalar.activation(r3[:], d3[:], ACT.Relu, scale=-2.0)
-            return d4, r3
+            return d3, d4
 
-        def b_sum(t, d4, r3):
-            nc.vector.scalar_tensor_tensor(z2_planes[:, t, :], d4[:], 0.0, r3[:], ALU.max, ALU.add)
+        def b_sum(t, d3, d4):
+            r3 = sb("r3_%d" % t, [P, N], F32)
+            nc.scalar.activation(r3[:], d3[:], ACT.Relu, scale=minus_gi[:, t : t + 1])
+            r4 = sb("r4_%d" % t, [P, N], F32)
+            nc.scalar.activation(r4[:], d4[:], ACT.Relu, scale=half_gi[:, t : t + 1])
+            for f in range(PACK):
+                cols = slice(f * P, (f + 1) * P)
+                dst = sum_bank[f][:, t * P : (t + 1) * P]
+                nc.tensor.matmul(dst, r3[:, cols], ident[:], start=True, stop=False, is_transpose=True)
+                nc.tensor.matmul(dst, r4[:, cols], ident[:], start=False, stop=True, is_transpose=True)
+
+        z2_turned = [sb("z2_turned%d" % f, [P, S], BF16) for f in range(PACK)]
+        z2_woven = sb("z2_woven", [P, PACK * N], BF16)
+
+        def z2_round(f):
+            nc.scalar.copy(
+                z2_turned[f][:].rearrange("c (u p e) -> c u p e", u=2, e=2),
+                sum_bank[f][:].rearrange("c (u e p) -> c u p e", u=2, e=2),
+            )
+
+        def z2_turn_back(h):
+            words = bank(PACK + h)
+            for g in range(2):
+                pairs = z2_turned[2 * h + g][:].bitcast(F32)
+                for u in range(2):
+                    nc.tensor.transpose(
+                        words[:, (2 * g + u) * P : (2 * g + u + 1) * P], pairs[:, u * P : (u + 1) * P], ident[:]
+                    )
+            return words
+
+        def z2_weave(h, words):
+            nc.scalar.copy(
+                z2_woven[:, h * 1024 : (h + 1) * 1024].bitcast(F32).rearrange("p (g c u) -> p g c u", g=2, u=2),
+                words[:].rearrange("p (g u c) -> p g c u", g=2, u=2),
+            )
 
         def a_out(t):
             nc.scalar.copy(a_win[t][:], a_acc[t][:])
@@ -184,43 +225,43 @@ def tile_picked_mombfoldhingesend_none_p_kernel(
         def a_fold(t, pa):
             nc.vector.tensor_tensor(a_win[t][:].indirect(n2_t[:]), pa[:], gate[t][:], ALU.mult)
 
-        def a_round(t):
+        def a_round(t, u0=0, u1=PACK):
             nc.scalar.activation(
-                z_planes[:, t, :].rearrange("p (u m) -> p m u", u=PACK),
-                a_win[t][:].rearrange("p (m u) -> p m u", u=PACK),
+                z_planes[:, t, :].rearrange("p (u m) -> p m u", u=PACK)[:, :, u0:u1],
+                a_win[t][:].rearrange("p (m u) -> p m u", u=PACK)[:, :, u0:u1],
                 ACT.Copy, scale=gts[:, t : t + 1],
             )
 
-        b_out(0)
-        b_out(1)
-        h0 = b_hinge(0)
-        b_out(2)
-        h1 = b_hinge(1)
-        b_sum(0, *h0)
-        b_out(3)
-        h2 = b_hinge(2)
-        b_sum(1, *h1)
+        a_acc = []
+        hinge = []
+        for t in range(PACK):
+            b_out(t)
+            a_acc.append(a_product(t))
+            hinge.append(b_hinge(t))
+            if t == 2:
+                b_sum(0, *hinge[0])
+        b_sum(1, *hinge[1])
         a_out(0)
-        h3 = b_hinge(3)
-        b_sum(2, *h2)
+        b_sum(2, *hinge[2])
         a_out(1)
-        p0 = a_pick(0)
-        b_sum(3, *h3)
-        a_fold(0, p0)
+        b_sum(3, *hinge[3])
         a_out(2)
-        p1 = a_pick(1)
-        a_out(3)
-        p2 = a_pick(2)
-        a_fold(1, p1)
-        z2_woven = sb("z2_woven", [P, PACK * N], BF16)
-        weave(nc.scalar.copy, z2_woven[:], z2_planes[:])
+        a_fold(0, a_pick(0))
+        a_fold(1, a_pick(1))
+        a_fold(2, a_pick(2))
+        for f in range(PACK):
+            z2_round(f)
+        words = [z2_turn_back(h) for h in range(2)]
         a_round(0)
+        a_out(3)
         p3 = a_pick(3)
-        a_fold(2, p2)
-        a_round(1)
         a_fold(3, p3)
+        a_round(1)
+        for h in range(2):
+            z2_weave(h, words[h])
         a_round(2)
-        a_round(3)
+        a_round(3, 0, 1)
+        a_round(3, 1, PACK)
         z2_codes = sb("z2_codes", [P, N], U32)
         z2_scales = sb("z2_scales", [P, N], U8)
         nc.vector.quantize_mx(z2_codes[:].bitcast(FP8X4), z2_scales[:], z2_woven[:])
@@ -236,13 +277,15 @@ def tile_picked_mombfoldhingesend_none_p_kernel(
         def moment(u, engine_copy):
             weave(engine_copy, z_woven[u][:], z_planes[:, :, u * P : (u + 1) * P])
             nc.vector.quantize_mx(z_codes[u][:].bitcast(FP8X4), z_scales[u][:], z_woven[u][:])
-            acc = psum.tile([P, N], F32, name="acc")
+            acc = bank(u)
             nc.tensor.matmul_mx(
                 acc[:], z_codes[u][:].bitcast(FP8X4), z_scales[u][:],
                 z2_codes[:].bitcast(FP8X4), z2_scales[:], start=True, stop=True,
             )
-            nc.scalar.activation(rl[u][:], acc[:], ACT.Relu, scale=0.0625)
             return acc
+
+        def positive(u, acc):
+            nc.scalar.activation(rl[u][:], acc[:], ACT.Relu, scale=0.0625)
 
         def halve(u, acc):
             nc.scalar.activation(less[u][:], acc[:], ACT.Copy, scale=-0.03125)
@@ -251,38 +294,36 @@ def tile_picked_mombfoldhingesend_none_p_kernel(
             nc.vector.tensor_copy(sent[u][:].indirect(n5_t[:]), rl[u][:])
 
         def finish_by_transposes(u):
-            turned = psum_turn.tile([P, N], F32, name="turn")
+            turned = bank(6)
             for c in range(PACK):
                 cols = slice(c * P, (c + 1) * P)
                 nc.tensor.matmul(turned[:, cols], less[u][:, cols], ident[:], start=True, stop=False, is_transpose=True)
                 nc.tensor.matmul(turned[:, cols], sent[u][:, cols], ident[:], start=False, stop=True, is_transpose=True)
             turned_sb = sb("turned%d" % u, [P, N], F32)
             nc.scalar.copy(turned_sb[:], turned[:])
-            back = psum_turn.tile([P, N], F32, name="turn")
+            back = bank(7)
             for c in range(PACK):
                 cols = slice(c * P, (c + 1) * P)
                 nc.tensor.transpose(back[:, cols], turned_sb[:, cols], ident[:])
             res = sb("res%d" % u, [P, N], F32)
             nc.scalar.copy(res[:], back[:])
-            nc.sync.dma_start(out_rows[:, u, :], res[:])
+            nc.scalar.dma_start(out_rows[:, u, :], res[:])
 
-        acc0 = moment(0, nc.vector.tensor_copy)
-        acc1 = moment(1, nc.vector.tensor_copy)
-        acc2 = moment(2, nc.vector.tensor_copy)
+        accs = [moment(u, nc.vector.tensor_copy) for u in range(PACK - 1)]
+        positive(0, accs[0])
         send(0)
-        halve(0, acc0)
-        acc3 = moment(3, nc.scalar.copy)
-        halve(1, acc1)
-        send(1)
-        finish_by_transposes(0)
-        halve(2, acc2)
-        halve(3, acc3)
-        send(2)
-        finish_by_transposes(1)
-        send(3)
-        finish_by_transposes(2)
+        accs.append(moment(PACK - 1, nc.scalar.copy))
+        positive(1, accs[1])
+        positive(2, accs[2])
+        for u in range(PACK - 1):
+            halve(u, accs[u])
+        positive(3, accs[3])
+        halve(3, accs[3])
+        for u in range(1, PACK):
+            send(u)
+            finish_by_transposes(u - 1)
         for h in range(2):
             cols = slice(h * 256, (h + 1) * 256)
             res = sb("res_last%d" % h, [P, 256], F32)
             nc.vector.tensor_tensor(res[:], sent[3][:, cols], less[3][:, cols], ALU.add)
-            (nc.sync if h == 0 else nc.scalar).dma_start(out_rows[:, 3, cols], res[:])
+            nc.sync.dma_start(out_rows[:, 3, cols], res[:])

@@ -49,6 +49,8 @@ def tile_picked_mombfoldhingesend_none_p_kernel(
         scale_table = sb("scale_table", [P, T], U8)
         nc.vector.memset(scale_table[:, :1280].bitcast(I32), 0)
         nc.gpsimd.memset(scale_table[:, 1280:].bitcast(I32), 0)
+        gates = sb("gates", [P, P], F32)
+        nc.vector.memset(gates[:], 0.0)
         nc.gpsimd.memset(warm[:, 0:1], 0.0)
         nc.scalar.activation(warm[:, 1:2], warm[:, 0:1], ACT.Sigmoid)
 
@@ -63,8 +65,6 @@ def tile_picked_mombfoldhingesend_none_p_kernel(
         nc.sync.dma_start(wb_raw[:], wb.rearrange("(p j) n -> p j n", j=PACK))
         word_table = sb("word_table", [P, T], I32)
         nc.sync.dma_start(word_table[:], x_words[0].rearrange("p c r -> p (c r)").bitcast(I32))
-        gates = sb("gates", [P, P], F32)
-        nc.gpsimd.memset(gates[:], 0.0)
         for row, src in ((0, gi), (PACK, gt)):
             nc.sync.dma_start(
                 gates[row : row + PACK, :].rearrange("t (g q) -> t g q", q=4),
@@ -82,25 +82,24 @@ def tile_picked_mombfoldhingesend_none_p_kernel(
         make_identity(nc, ident[:])
         gates_turned = bank(7)
         nc.tensor.transpose(gates_turned[:, :P], gates[:], ident[:])
-        gates_t = sb("gates_t", [P, 2 * PACK], F32)
-        nc.scalar.copy(gates_t[:], gates_turned[:, : 2 * PACK])
-        gi_t = gates_t[:, :PACK]
-        gt_t = gates_t[:, PACK:]
+        gi_t = gates_turned[:, :PACK]
+        gt_t = gates_turned[:, PACK : 2 * PACK]
 
         b_win = [sb("b_win%d" % t, [P, 2 * N], F32) for t in range(PACK)]
         for t in range(PACK):
-            nc.gpsimd.memset(b_win[t][:, N:], 0.0)
+            nc.vector.memset(b_win[t][:, N:], 0.0)
 
-        sgn = sb("sgn", [P, PACK], F32)
-        nc.gpsimd.tensor_scalar(sgn[:], gi_t, 0.0, -0.5, ALU.is_ge, ALU.add)
         half_gi = sb("half_gi", [P, PACK], F32)
-        nc.gpsimd.tensor_tensor(half_gi[:], gi_t, sgn[:], ALU.mult)
+        nc.scalar.activation(half_gi[:], gi_t, ACT.Abs, scale=0.5)
+        sign0 = sb("sign0", [P, PACK], F32)
+        nc.scalar.activation(sign0[:], gi_t, ACT.Sign)
         minus_gi = sb("minus_gi", [P, PACK], F32)
-        nc.gpsimd.tensor_scalar(minus_gi[:], half_gi[:], -2.0, 0.0, ALU.mult, ALU.add)
-        gt2 = sb("gt2", [P, PACK], F32)
-        nc.gpsimd.tensor_scalar(gt2[:], gt_t, 2.0, 0.0, ALU.mult, ALU.add)
+        nc.scalar.activation(minus_gi[:], half_gi[:], ACT.Copy, scale=-2.0)
+        sign = sb("sign", [P, PACK], F32)
+        nc.scalar.activation(sign[:], sign0[:], ACT.Sign, bias=0.5)
         gts = sb("gts", [P, PACK], F32)
-        nc.gpsimd.tensor_tensor(gts[:], gt2[:], sgn[:], ALU.mult)
+        for t in range(PACK):
+            nc.scalar.activation(gts[:, t : t + 1], gt_t[:, t : t + 1], ACT.Copy, scale=sign[:, t : t + 1])
 
         def pick_scales(name, lst):
             plain = sb(name + "_plain", [P, S], U8)
@@ -238,8 +237,7 @@ def tile_picked_mombfoldhingesend_none_p_kernel(
             b_out(t)
             a_acc.append(a_product(t))
             hinge.append(b_hinge(t))
-            if t == 2:
-                b_sum(0, *hinge[0])
+        b_sum(0, *hinge[0])
         b_sum(1, *hinge[1])
         a_out(0)
         b_sum(2, *hinge[2])

@@ -4,7 +4,7 @@ import concourse.mybir as mybir
 from concourse.masks import make_identity
 
 K, T, S, H, N, W = 512, 2048, 512, 512, 512, 256
-FLOPS = 3 * 2 * 512 * 512 * 512
+FLOPS = 2 * K * S * H + 2 * K * S * N + 2 * S * H * N
 
 F32 = mybir.dt.float32
 BF16 = mybir.dt.bfloat16
@@ -18,6 +18,14 @@ ACT = mybir.ActivationFunctionType
 
 P = 128
 PACK = 4
+RUN = 4
+LINE = 4
+QUADRANTS = 4
+VECTOR_ZEROES = 1280
+SCALAR_COPIES = 2
+SUM_BANK = 4
+TURNED_BANK, BACK_BANK = 6, 7
+LAST = PACK - 1
 
 
 def tile_picked_mombfoldhingesend_none_p_kernel(
@@ -31,297 +39,297 @@ def tile_picked_mombfoldhingesend_none_p_kernel(
         def bank(n):
             return psum.tile([P, N], F32, name="bank%d" % n)
 
-        def sb(name, shape, dtype, tag=None):
-            return keep.tile(shape, dtype, name=name, tag=tag or name, align_bytes=64)
+        def sbuf(name, shape, dtype):
+            return keep.tile(shape, dtype, name=name, align_bytes=64)
 
         def load_list(name, src):
-            tile = sb(name, list(src.shape), U16)
+            tile = sbuf(name, list(src.shape), U16)
             nc.sync.dma_start(tile[:], src)
             return tile
 
-        def weave(engine_copy, dst, src):
-            engine_copy(
-                dst.rearrange("p (c i t) -> p c t i", i=4, t=PACK),
-                src.rearrange("p t (c i) -> p c t i", i=4),
+        def block(n):
+            return slice(n * P, (n + 1) * P)
+
+        def weave(copy, dst, src):
+            copy(
+                dst.rearrange("p (c i t) -> p c t i", i=LINE, t=PACK),
+                src.rearrange("p t (c i) -> p c t i", i=LINE),
             )
 
-        warm = sb("warm", [P, 2], F32)
-        scale_table = sb("scale_table", [P, T], U8)
-        nc.vector.memset(scale_table[:, :1280].bitcast(I32), 0)
-        nc.gpsimd.memset(scale_table[:, 1280:].bitcast(I32), 0)
-        gates = sb("gates", [P, P], F32)
+        def product(n, left_words, left_scales, right_words, right_scales):
+            acc = bank(n)
+            nc.tensor.matmul_mx(
+                acc[:], left_words.bitcast(FP8X4), left_scales, right_words.bitcast(FP8X4), right_scales,
+                start=True, stop=True,
+            )
+            return acc
+
+        def transposed_sum(dst, first, second):
+            nc.tensor.matmul(dst, first, ident[:], start=True, stop=False, is_transpose=True)
+            nc.tensor.matmul(dst, second, ident[:], start=False, stop=True, is_transpose=True)
+
+        zero_half = sbuf("zero_half", [P, 2], F32)
+        scale_table = sbuf("scale_table", [P, T], U8)
+        nc.vector.memset(scale_table[:, :VECTOR_ZEROES].bitcast(I32), 0)
+        nc.gpsimd.memset(scale_table[:, VECTOR_ZEROES:].bitcast(I32), 0)
+        gates = sbuf("gates", [P, P], F32)
         nc.vector.memset(gates[:], 0.0)
-        nc.gpsimd.memset(warm[:, 0:1], 0.0)
-        nc.scalar.activation(warm[:, 1:2], warm[:, 0:1], ACT.Sigmoid)
+        nc.gpsimd.memset(zero_half[:, 0:1], 0.0)
+        nc.scalar.activation(zero_half[:, 1:2], zero_half[:, 0:1], ACT.Sigmoid)
 
-        two_t = load_list("two_t", two)
-        offs_t = load_list("offs_t", offs)
-        for q in range(4):
+        two_list = load_list("two_list", two)
+        offs_list = load_list("offs_list", offs)
+        for quadrant in range(QUADRANTS):
             nc.sync.dma_start(
-                scale_table[32 * q : 32 * q + 4, :].bitcast(I32),
-                x_scales[0, 4 * q : 4 * q + 4, :].bitcast(I32),
+                scale_table[32 * quadrant : 32 * quadrant + 4, :].bitcast(I32),
+                x_scales[0, 4 * quadrant : 4 * quadrant + 4, :].bitcast(I32),
             )
-        wb_raw = sb("wb_raw", [P, PACK, N], F32)
+        wb_raw = sbuf("wb_raw", [P, PACK, N], F32)
         nc.sync.dma_start(wb_raw[:], wb.rearrange("(p j) n -> p j n", j=PACK))
-        word_table = sb("word_table", [P, T], I32)
+        word_table = sbuf("word_table", [P, T], I32)
         nc.sync.dma_start(word_table[:], x_words[0].rearrange("p c r -> p (c r)").bitcast(I32))
         for row, src in ((0, gi), (PACK, gt)):
             nc.sync.dma_start(
-                gates[row : row + PACK, :].rearrange("t (g q) -> t g q", q=4),
-                src.rearrange("(g t q) o -> t g (q o)", t=PACK, q=4),
+                gates[row : row + PACK, :].rearrange("t (g q) -> t g q", q=RUN),
+                src.rearrange("(g t q) o -> t g (q o)", t=PACK, q=RUN),
             )
-        wa_raw = sb("wa_raw", [P, PACK, H], F32)
+        wa_raw = sbuf("wa_raw", [P, PACK, H], F32)
         nc.sync.dma_start(wa_raw[:], wa.rearrange("(p j) n -> p j n", j=PACK))
-        n3_t = load_list("n3_t", n3)
-        n4_t = load_list("n4_t", n4)
-        n1_t = load_list("n1_t", n1)
-        n2_t = load_list("n2_t", n2)
-        n5_t = load_list("n5_t", n5)
+        n3_list = load_list("n3_list", n3)
+        n4_list = load_list("n4_list", n4)
+        n1_list = load_list("n1_list", n1)
+        n2_list = load_list("n2_list", n2)
+        n5_list = load_list("n5_list", n5)
 
-        ident = sb("ident", [P, P], F32)
+        ident = sbuf("ident", [P, P], F32)
         make_identity(nc, ident[:])
-        gates_turned = bank(7)
+        gates_turned = bank(BACK_BANK)
         nc.tensor.transpose(gates_turned[:, :P], gates[:], ident[:])
-        gi_t = gates_turned[:, :PACK]
-        gt_t = gates_turned[:, PACK : 2 * PACK]
+        gi_slots = gates_turned[:, :PACK]
+        gt_slots = gates_turned[:, PACK : 2 * PACK]
 
-        b_win = [sb("b_win%d" % t, [P, 2 * N], F32) for t in range(PACK)]
+        b_window = [sbuf("b_window%d" % t, [P, 2 * N], F32) for t in range(PACK)]
         for t in range(PACK):
-            nc.vector.memset(b_win[t][:, N:], 0.0)
+            nc.vector.memset(b_window[t][:, N:], 0.0)
 
-        half_gi = sb("half_gi", [P, PACK], F32)
-        nc.scalar.activation(half_gi[:], gi_t, ACT.Abs, scale=0.5)
-        sign0 = sb("sign0", [P, PACK], F32)
-        nc.scalar.activation(sign0[:], gi_t, ACT.Sign)
-        minus_gi = sb("minus_gi", [P, PACK], F32)
+        half_gi = sbuf("half_gi", [P, PACK], F32)
+        nc.scalar.activation(half_gi[:], gi_slots, ACT.Abs, scale=0.5)
+        sign_or_zero = sbuf("sign_or_zero", [P, PACK], F32)
+        nc.scalar.activation(sign_or_zero[:], gi_slots, ACT.Sign)
+        minus_gi = sbuf("minus_gi", [P, PACK], F32)
         nc.scalar.activation(minus_gi[:], half_gi[:], ACT.Copy, scale=-2.0)
-        sign = sb("sign", [P, PACK], F32)
-        nc.scalar.activation(sign[:], sign0[:], ACT.Sign, bias=0.5)
-        gts = sb("gts", [P, PACK], F32)
+        sign = sbuf("sign", [P, PACK], F32)
+        nc.scalar.activation(sign[:], sign_or_zero[:], ACT.Sign, bias=zero_half[:, 1:2])
+        signed_gt = sbuf("signed_gt", [P, PACK], F32)
         for t in range(PACK):
-            nc.scalar.activation(gts[:, t : t + 1], gt_t[:, t : t + 1], ACT.Copy, scale=sign[:, t : t + 1])
+            nc.scalar.activation(signed_gt[:, t : t + 1], gt_slots[:, t : t + 1], ACT.Copy, scale=sign[:, t : t + 1])
 
-        def pick_scales(name, lst):
-            plain = sb(name + "_plain", [P, S], U8)
-            nc.vector.tensor_copy(plain[:], scale_table[:].indirect(lst[:]))
-            dealt = sb(name + "_dealt", [P, S], U8)
+        def pick_scales(name, offsets):
+            picked = sbuf(name, [P, S], U8)
+            nc.vector.tensor_copy(picked[:], scale_table[:].indirect(offsets[:]))
+            return picked
+
+        def deal_scales(name, picked):
+            dealt = sbuf(name, [P, S], U8)
             nc.vector.tensor_copy(
                 dealt[:].bitcast(I32).rearrange("p (t g) -> p t g", t=PACK),
-                plain[:].bitcast(I32).rearrange("p (g t) -> p t g", t=PACK),
+                picked[:].bitcast(I32).rearrange("p (g t) -> p t g", t=PACK),
             )
             return dealt
 
-        def pick_words(name, lst, tag=None):
-            dealt = sb(name, [P, S], U32, tag)
+        def pick_words(name, offsets):
+            dealt = sbuf(name, [P, S], U32)
             nc.vector.tensor_copy(
-                dealt[:].rearrange("p (t g q) -> p g t q", t=PACK, q=4),
-                word_table[:].bitcast(U32).indirect(lst[:]),
+                dealt[:].rearrange("p (t g q) -> p g t q", t=PACK, q=RUN),
+                word_table[:].bitcast(U32).indirect(offsets[:]),
             )
             return dealt
 
-        xb_scales = pick_scales("xb_scales", two_t)
-        xa_scales = pick_scales("xa_scales", offs_t)
-        wb_codes = sb("wb_codes", [P, N], U32)
-        wb_scales = sb("wb_scales", [P, N], U8)
-        wb_woven = sb("wb_woven", [P, PACK * N], BF16)
-        weave(nc.scalar.copy, wb_woven[:, :1024], wb_raw[:, :, :256])
-        weave(nc.vector.tensor_copy, wb_woven[:, 1024:], wb_raw[:, :, 256:])
-        nc.vector.quantize_mx(wb_codes[:].bitcast(FP8X4), wb_scales[:], wb_woven[:])
-        xb_words = pick_words("xb_words", two_t)
+        xb_picked = pick_scales("xb_picked", two_list)
+        xa_picked = pick_scales("xa_picked", offs_list)
+        xb_scales = deal_scales("xb_scales", xb_picked)
+        xa_scales = deal_scales("xa_scales", xa_picked)
+        wb_words = sbuf("wb_words", [P, N], U32)
+        wb_scales = sbuf("wb_scales", [P, N], U8)
+        wb_woven = sbuf("wb_woven", [P, PACK * N], BF16)
+        weave(nc.scalar.copy, wb_woven[:, : PACK * N // 2], wb_raw[:, :, : N // 2])
+        weave(nc.vector.tensor_copy, wb_woven[:, PACK * N // 2 :], wb_raw[:, :, N // 2 :])
+        nc.vector.quantize_mx(wb_words[:].bitcast(FP8X4), wb_scales[:], wb_woven[:])
+        xb_words = pick_words("xb_words", two_list)
+        b_acc = [
+            product(t, xb_words[:, block(t)], xb_scales[:, block(t)], wb_words[:], wb_scales[:]) for t in range(PACK)
+        ]
 
-        b_acc = []
-        for t in range(PACK):
-            acc = bank(t)
-            rows = slice(t * P, (t + 1) * P)
-            nc.tensor.matmul_mx(
-                acc[:], xb_words[:, rows].bitcast(FP8X4), xb_scales[:, rows],
-                wb_codes[:].bitcast(FP8X4), wb_scales[:], start=True, stop=True,
-            )
-            b_acc.append(acc)
-
-        xa_words = pick_words("xa_words", offs_t)
-        wa_woven = sb("wa_woven", [P, PACK * H], BF16)
+        xa_words = pick_words("xa_words", offs_list)
+        wa_woven = sbuf("wa_woven", [P, PACK * H], BF16)
         weave(nc.vector.tensor_copy, wa_woven[:], wa_raw[:])
-        wa_codes = sb("wa_codes", [P, H], U32)
-        wa_scales = sb("wa_scales", [P, H], U8)
-        nc.vector.quantize_mx(wa_codes[:].bitcast(FP8X4), wa_scales[:], wa_woven[:])
+        wa_words = sbuf("wa_words", [P, H], U32)
+        wa_scales = sbuf("wa_scales", [P, H], U8)
 
-        def a_product(t):
-            acc = bank(t)
-            rows = slice(t * P, (t + 1) * P)
-            nc.tensor.matmul_mx(
-                acc[:], xa_words[:, rows].bitcast(FP8X4), xa_scales[:, rows],
-                wa_codes[:].bitcast(FP8X4), wa_scales[:], start=True, stop=True,
-            )
-            return acc
-
-        b_plain = [sb("b_plain%d" % t, [P, N], F32) for t in range(PACK)]
-        a_win = [sb("a_win%d" % t, [P, H], F32) for t in range(PACK)]
-        gate = [sb("gate%d" % t, [P, W], F32) for t in range(PACK)]
-        z_planes = sb("z_planes", [P, PACK, H], BF16)
+        b_plain = [sbuf("b_plain%d" % t, [P, N], F32) for t in range(PACK)]
+        a_window = [sbuf("a_window%d" % t, [P, H], F32) for t in range(PACK)]
+        gate = [sbuf("gate%d" % t, [P, W], F32) for t in range(PACK)]
+        z_slots = sbuf("z_slots", [P, PACK, H], BF16)
 
         def b_out(t):
-            nc.scalar.copy(b_win[t][:, :N], b_acc[t][:])
-            if t < 2:
+            nc.scalar.copy(b_window[t][:, :N], b_acc[t][:])
+            if t < SCALAR_COPIES:
                 nc.scalar.copy(b_plain[t][:], b_acc[t][:])
             else:
-                nc.sync.dma_start(b_plain[t][:], b_win[t][:, :N])
+                nc.sync.dma_start(b_plain[t][:], b_window[t][:, :N])
 
-        sum_bank = [bank(PACK + f) for f in range(PACK)]
+        z2_sum = [bank(SUM_BANK + f) for f in range(PACK)]
 
-        def b_hinge(t):
-            d3 = sb("d3_%d" % t, [P, N], F32)
-            nc.vector.tensor_tensor(d3[:], b_win[t][:].indirect(n3_t[:]), b_plain[t][:], ALU.subtract)
-            d4 = sb("d4_%d" % t, [P, N], F32)
-            nc.vector.tensor_tensor(d4[:], b_win[t][:].indirect(n4_t[:]), b_plain[t][:], ALU.subtract)
+        def b_differences(t):
+            d3 = sbuf("d3_%d" % t, [P, N], F32)
+            nc.vector.tensor_tensor(d3[:], b_window[t][:].indirect(n3_list[:]), b_plain[t][:], ALU.subtract)
+            d4 = sbuf("d4_%d" % t, [P, N], F32)
+            nc.vector.tensor_tensor(d4[:], b_window[t][:].indirect(n4_list[:]), b_plain[t][:], ALU.subtract)
             return d3, d4
 
-        def b_sum(t, d3, d4):
-            r3 = sb("r3_%d" % t, [P, N], F32)
+        def z2_add(t, d3, d4):
+            r3 = sbuf("r3_%d" % t, [P, N], F32)
             nc.scalar.activation(r3[:], d3[:], ACT.Relu, scale=minus_gi[:, t : t + 1])
-            r4 = sb("r4_%d" % t, [P, N], F32)
+            r4 = sbuf("r4_%d" % t, [P, N], F32)
             nc.scalar.activation(r4[:], d4[:], ACT.Relu, scale=half_gi[:, t : t + 1])
             for f in range(PACK):
-                cols = slice(f * P, (f + 1) * P)
-                dst = sum_bank[f][:, t * P : (t + 1) * P]
-                nc.tensor.matmul(dst, r3[:, cols], ident[:], start=True, stop=False, is_transpose=True)
-                nc.tensor.matmul(dst, r4[:, cols], ident[:], start=False, stop=True, is_transpose=True)
+                transposed_sum(z2_sum[f][:, block(t)], r3[:, block(f)], r4[:, block(f)])
 
-        z2_turned = [sb("z2_turned%d" % f, [P, S], BF16) for f in range(PACK)]
-        z2_woven = sb("z2_woven", [P, PACK * N], BF16)
+        z2_turned = [sbuf("z2_turned%d" % f, [P, S], BF16) for f in range(PACK)]
+        z2_woven = sbuf("z2_woven", [P, PACK * N], BF16)
 
         def z2_round(f):
             nc.scalar.copy(
-                z2_turned[f][:].rearrange("c (u p e) -> c u p e", u=2, e=2),
-                sum_bank[f][:].rearrange("c (u e p) -> c u p e", u=2, e=2),
+                z2_turned[f][:].rearrange("c (v p e) -> c v p e", v=2, e=2),
+                z2_sum[f][:].rearrange("c (v e p) -> c v p e", v=2, e=2),
             )
 
         def z2_turn_back(h):
-            words = bank(PACK + h)
-            for g in range(2):
-                pairs = z2_turned[2 * h + g][:].bitcast(F32)
-                for u in range(2):
-                    nc.tensor.transpose(
-                        words[:, (2 * g + u) * P : (2 * g + u + 1) * P], pairs[:, u * P : (u + 1) * P], ident[:]
-                    )
-            return words
+            pairs_back = bank(SUM_BANK + h)
+            for s in range(2):
+                pairs = z2_turned[2 * h + s][:].bitcast(F32)
+                for v in range(2):
+                    nc.tensor.transpose(pairs_back[:, block(2 * s + v)], pairs[:, block(v)], ident[:])
+            return pairs_back
 
-        def z2_weave(h, words):
+        def z2_weave(h, pairs_back):
+            half = slice(h * PACK * N // 2, (h + 1) * PACK * N // 2)
             nc.scalar.copy(
-                z2_woven[:, h * 1024 : (h + 1) * 1024].bitcast(F32).rearrange("p (g c u) -> p g c u", g=2, u=2),
-                words[:].rearrange("p (g u c) -> p g c u", g=2, u=2),
+                z2_woven[:, half].bitcast(F32).rearrange("p (s c v) -> p s c v", s=2, v=2),
+                pairs_back[:].rearrange("p (s v c) -> p s c v", s=2, v=2),
             )
 
         def a_out(t):
-            nc.scalar.copy(a_win[t][:], a_acc[t][:])
-            nc.scalar.activation(gate[t][:], a_win[t][:].indirect(n2_t[:]), ACT.Sigmoid)
+            nc.scalar.copy(a_window[t][:], a_acc[t][:])
+
+        def a_gate(t):
+            nc.scalar.activation(gate[t][:], a_window[t][:].indirect(n2_list[:]), ACT.Sigmoid)
 
         def a_pick(t):
-            pa = sb("pa%d" % t, [P, W], F32)
-            nc.vector.tensor_copy(pa[:], a_win[t][:].indirect(n1_t[:]))
+            pa = sbuf("pa%d" % t, [P, W], F32)
+            nc.vector.tensor_copy(pa[:], a_window[t][:].indirect(n1_list[:]))
             return pa
 
         def a_fold(t, pa):
-            nc.vector.tensor_tensor(a_win[t][:].indirect(n2_t[:]), pa[:], gate[t][:], ALU.mult)
+            nc.vector.tensor_tensor(a_window[t][:].indirect(n2_list[:]), pa[:], gate[t][:], ALU.mult)
 
-        def a_round(t, u0=0, u1=PACK):
+        def z_round(t, first, end):
             nc.scalar.activation(
-                z_planes[:, t, :].rearrange("p (u m) -> p m u", u=PACK)[:, :, u0:u1],
-                a_win[t][:].rearrange("p (m u) -> p m u", u=PACK)[:, :, u0:u1],
-                ACT.Copy, scale=gts[:, t : t + 1],
+                z_slots[:, t, :].rearrange("p (u m) -> p m u", u=PACK)[:, :, first:end],
+                a_window[t][:].rearrange("p (m u) -> p m u", u=PACK)[:, :, first:end],
+                ACT.Copy, scale=signed_gt[:, t : t + 1],
             )
 
-        a_acc = []
-        hinge = []
+        differences = []
         for t in range(PACK):
             b_out(t)
-            a_acc.append(a_product(t))
-            hinge.append(b_hinge(t))
-        b_sum(0, *hinge[0])
-        b_sum(1, *hinge[1])
-        a_out(0)
-        b_sum(2, *hinge[2])
-        a_out(1)
-        b_sum(3, *hinge[3])
-        a_out(2)
-        a_fold(0, a_pick(0))
-        a_fold(1, a_pick(1))
-        a_fold(2, a_pick(2))
+            differences.append(b_differences(t))
+            if t == 0:
+                nc.vector.quantize_mx(wa_words[:].bitcast(FP8X4), wa_scales[:], wa_woven[:])
+        a_acc = [
+            product(t, xa_words[:, block(t)], xa_scales[:, block(t)], wa_words[:], wa_scales[:]) for t in range(PACK)
+        ]
+        pa_slots = []
+        for t in range(PACK):
+            z2_add(t, *differences[t])
+            a_out(t)
+            pa_slots.append(a_pick(t))
+            if t > 0:
+                a_gate(t - 1)
+                a_fold(t - 1, pa_slots[t - 1])
         for f in range(PACK):
             z2_round(f)
-        words = [z2_turn_back(h) for h in range(2)]
-        a_round(0)
-        a_out(3)
-        p3 = a_pick(3)
-        a_fold(3, p3)
-        a_round(1)
+        z2_pairs = [z2_turn_back(h) for h in range(2)]
+        a_gate(LAST)
+        a_fold(LAST, pa_slots[LAST])
+        z_round(0, 0, PACK)
+        z_round(1, 0, PACK)
         for h in range(2):
-            z2_weave(h, words[h])
-        a_round(2)
-        a_round(3, 0, 1)
-        a_round(3, 1, PACK)
-        z2_codes = sb("z2_codes", [P, N], U32)
-        z2_scales = sb("z2_scales", [P, N], U8)
-        nc.vector.quantize_mx(z2_codes[:].bitcast(FP8X4), z2_scales[:], z2_woven[:])
+            z2_weave(h, z2_pairs[h])
+        z_round(2, 0, PACK)
+        z_round(LAST, 0, 1)
+        z_round(LAST, 1, PACK)
+        z2_words = sbuf("z2_words", [P, N], U32)
+        z2_scales = sbuf("z2_scales", [P, N], U8)
+        nc.vector.quantize_mx(z2_words[:].bitcast(FP8X4), z2_scales[:], z2_woven[:])
 
-        z_codes = [sb("z_codes%d" % u, [P, P], U32) for u in range(PACK)]
-        z_scales = [sb("z_scales%d" % u, [P, P], U8) for u in range(PACK)]
-        z_woven = [sb("z_woven%d" % u, [P, PACK * P], BF16) for u in range(PACK)]
-        out_rows = out.rearrange("(p u) n -> p u n", u=PACK)
-        sent = [sb("sent%d" % u, [P, 2 * N], F32) for u in range(PACK)]
-        less = [sb("less%d" % u, [P, N], F32) for u in range(PACK)]
-        rl = [sb("rl%d" % u, [P, N], F32) for u in range(PACK)]
+        z_words = [sbuf("z_words%d" % u, [P, P], U32) for u in range(PACK)]
+        z_scales = [sbuf("z_scales%d" % u, [P, P], U8) for u in range(PACK)]
+        z_woven = [sbuf("z_woven%d" % u, [P, PACK * P], BF16) for u in range(PACK)]
+        out_rows = out.rearrange("(m u) n -> m u n", u=PACK)
+        ds2 = [sbuf("ds2_%d" % u, [P, 2 * N], F32) for u in range(PACK)]
+        minus_half_cv = [sbuf("minus_half_cv%d" % u, [P, N], F32) for u in range(PACK)]
+        rl = [sbuf("rl%d" % u, [P, N], F32) for u in range(PACK)]
 
-        def moment(u, engine_copy):
-            weave(engine_copy, z_woven[u][:], z_planes[:, :, u * P : (u + 1) * P])
-            nc.vector.quantize_mx(z_codes[u][:].bitcast(FP8X4), z_scales[u][:], z_woven[u][:])
-            acc = bank(u)
-            nc.tensor.matmul_mx(
-                acc[:], z_codes[u][:].bitcast(FP8X4), z_scales[u][:],
-                z2_codes[:].bitcast(FP8X4), z2_scales[:], start=True, stop=True,
-            )
-            return acc
+        def z_weave(u, copy):
+            weave(copy, z_woven[u][:], z_slots[:, :, block(u)])
 
-        def positive(u, acc):
-            nc.scalar.activation(rl[u][:], acc[:], ACT.Relu, scale=0.0625)
+        def moment(u):
+            nc.vector.quantize_mx(z_words[u][:].bitcast(FP8X4), z_scales[u][:], z_woven[u][:])
+            return product(u, z_words[u][:], z_scales[u][:], z2_words[:], z2_scales[:])
 
-        def halve(u, acc):
-            nc.scalar.activation(less[u][:], acc[:], ACT.Copy, scale=-0.03125)
+        def rl_out(u):
+            nc.scalar.activation(rl[u][:], cv_acc[u][:], ACT.Relu, scale=0.0625)
+
+        def half_out(u):
+            nc.scalar.activation(minus_half_cv[u][:], cv_acc[u][:], ACT.Copy, scale=-0.5 * 0.0625)
 
         def send(u):
-            nc.vector.tensor_copy(sent[u][:].indirect(n5_t[:]), rl[u][:])
+            nc.vector.tensor_copy(ds2[u][:].indirect(n5_list[:]), rl[u][:])
 
         def finish_by_transposes(u):
-            turned = bank(6)
+            turned_acc = bank(TURNED_BANK)
             for c in range(PACK):
-                cols = slice(c * P, (c + 1) * P)
-                nc.tensor.matmul(turned[:, cols], less[u][:, cols], ident[:], start=True, stop=False, is_transpose=True)
-                nc.tensor.matmul(turned[:, cols], sent[u][:, cols], ident[:], start=False, stop=True, is_transpose=True)
-            turned_sb = sb("turned%d" % u, [P, N], F32)
-            nc.scalar.copy(turned_sb[:], turned[:])
-            back = bank(7)
+                transposed_sum(turned_acc[:, block(c)], minus_half_cv[u][:, block(c)], ds2[u][:, block(c)])
+            turned = sbuf("turned%d" % u, [P, N], F32)
+            nc.scalar.copy(turned[:], turned_acc[:])
+            back_acc = bank(BACK_BANK)
             for c in range(PACK):
-                cols = slice(c * P, (c + 1) * P)
-                nc.tensor.transpose(back[:, cols], turned_sb[:, cols], ident[:])
-            res = sb("res%d" % u, [P, N], F32)
-            nc.scalar.copy(res[:], back[:])
-            nc.scalar.dma_start(out_rows[:, u, :], res[:])
+                nc.tensor.transpose(back_acc[:, block(c)], turned[:, block(c)], ident[:])
+            result = sbuf("result%d" % u, [P, N], F32)
+            nc.scalar.copy(result[:], back_acc[:])
+            nc.scalar.dma_start(out_rows[:, u, :], result[:])
 
-        accs = [moment(u, nc.vector.tensor_copy) for u in range(PACK - 1)]
-        positive(0, accs[0])
+        z_weave(0, nc.vector.tensor_copy)
+        cv_acc = [moment(0)]
+        z_weave(1, nc.vector.tensor_copy)
+        z_weave(2, nc.vector.tensor_copy)
+        cv_acc.extend([moment(1), moment(2)])
+        rl_out(0)
         send(0)
-        accs.append(moment(PACK - 1, nc.scalar.copy))
-        positive(1, accs[1])
-        positive(2, accs[2])
-        for u in range(PACK - 1):
-            halve(u, accs[u])
-        positive(3, accs[3])
-        halve(3, accs[3])
+        z_weave(LAST, nc.scalar.copy)
+        cv_acc.append(moment(LAST))
+        rl_out(1)
+        rl_out(2)
+        for u in range(LAST):
+            half_out(u)
+        rl_out(LAST)
+        half_out(LAST)
         for u in range(1, PACK):
             send(u)
             finish_by_transposes(u - 1)
         for h in range(2):
-            cols = slice(h * 256, (h + 1) * 256)
-            res = sb("res_last%d" % h, [P, 256], F32)
-            nc.vector.tensor_tensor(res[:], sent[3][:, cols], less[3][:, cols], ALU.add)
-            nc.sync.dma_start(out_rows[:, 3, cols], res[:])
+            half = slice(h * N // 2, (h + 1) * N // 2)
+            result = sbuf("result_last%d" % h, [P, N // 2], F32)
+            nc.vector.tensor_tensor(result[:], ds2[LAST][:, half], minus_half_cv[LAST][:, half], ALU.add)
+            nc.sync.dma_start(out_rows[:, LAST, half], result[:])

from contextlib import ExitStack

import concourse.mybir as mybir
from concourse.masks import make_identity

K, T, S, H, N, W = 512, 2048, 512, 512, 512, 256
FLOPS = 2 * K * S * H + 2 * K * S * N + 2 * S * H * N

F32 = mybir.dt.float32
BF16 = mybir.dt.bfloat16
I32 = mybir.dt.int32
U32 = mybir.dt.uint32
U16 = mybir.dt.uint16
U8 = mybir.dt.uint8
FP8X4 = mybir.dt.float8_e4m3fn_x4
ALU = mybir.AluOpType
ACT = mybir.ActivationFunctionType

P = 128
PACK = 4
RUN = 4
LINE = 4
QUADRANTS = 4
VECTOR_ZEROES = 1280
SCALAR_COPIES = 2
SUM_BANK = 4
TURNED_BANK, BACK_BANK = 6, 7
LAST = PACK - 1


def tile_picked_mombfoldhingesend_none_p_kernel(
    tc, x_words, x_scales, wa, wb, gt, gi, offs, two, n1, n2, n3, n4, n5, out
):
    nc = tc.nc
    with ExitStack() as ctx:
        keep = ctx.enter_context(tc.tile_pool(name="keep", bufs=1))
        psum = ctx.enter_context(tc.psum_pool(name="psum", bufs=1))

        def bank(n):
            return psum.tile([P, N], F32, name="bank%d" % n)

        def sbuf(name, shape, dtype):
            return keep.tile(shape, dtype, name=name, align_bytes=64)

        def load_list(name, src):
            tile = sbuf(name, list(src.shape), U16)
            nc.sync.dma_start(tile[:], src)
            return tile

        def block(n):
            return slice(n * P, (n + 1) * P)

        def weave(copy, dst, src):
            copy(
                dst.rearrange("p (c i t) -> p c t i", i=LINE, t=PACK),
                src.rearrange("p t (c i) -> p c t i", i=LINE),
            )

        def product(n, left_words, left_scales, right_words, right_scales):
            acc = bank(n)
            nc.tensor.matmul_mx(
                acc[:], left_words.bitcast(FP8X4), left_scales, right_words.bitcast(FP8X4), right_scales,
                start=True, stop=True,
            )
            return acc

        def transposed_sum(dst, first, second):
            nc.tensor.matmul(dst, first, ident[:], start=True, stop=False, is_transpose=True)
            nc.tensor.matmul(dst, second, ident[:], start=False, stop=True, is_transpose=True)

        zero_half = sbuf("zero_half", [P, 2], F32)
        scale_table = sbuf("scale_table", [P, T], U8)
        nc.vector.memset(scale_table[:, :VECTOR_ZEROES].bitcast(I32), 0)
        nc.gpsimd.memset(scale_table[:, VECTOR_ZEROES:].bitcast(I32), 0)
        gates = sbuf("gates", [P, P], F32)
        nc.vector.memset(gates[:], 0.0)
        nc.gpsimd.memset(zero_half[:, 0:1], 0.0)
        nc.scalar.activation(zero_half[:, 1:2], zero_half[:, 0:1], ACT.Sigmoid)

        two_list = load_list("two_list", two)
        offs_list = load_list("offs_list", offs)
        for quadrant in range(QUADRANTS):
            nc.sync.dma_start(
                scale_table[32 * quadrant : 32 * quadrant + 4, :].bitcast(I32),
                x_scales[0, 4 * quadrant : 4 * quadrant + 4, :].bitcast(I32),
            )
        wb_raw = sbuf("wb_raw", [P, PACK, N], F32)
        nc.sync.dma_start(wb_raw[:], wb.rearrange("(p j) n -> p j n", j=PACK))
        word_table = sbuf("word_table", [P, T], I32)
        nc.sync.dma_start(word_table[:], x_words[0].rearrange("p c r -> p (c r)").bitcast(I32))
        for row, src in ((0, gi), (PACK, gt)):
            nc.sync.dma_start(
                gates[row : row + PACK, :].rearrange("t (g q) -> t g q", q=RUN),
                src.rearrange("(g t q) o -> t g (q o)", t=PACK, q=RUN),
            )
        wa_raw = sbuf("wa_raw", [P, PACK, H], F32)
        nc.sync.dma_start(wa_raw[:], wa.rearrange("(p j) n -> p j n", j=PACK))
        n3_list = load_list("n3_list", n3)
        n4_list = load_list("n4_list", n4)
        n1_list = load_list("n1_list", n1)
        n2_list = load_list("n2_list", n2)
        n5_list = load_list("n5_list", n5)

        ident = sbuf("ident", [P, P], F32)
        make_identity(nc, ident[:])
        gates_turned = bank(BACK_BANK)
        nc.tensor.transpose(gates_turned[:, :P], gates[:], ident[:])
        gi_slots = gates_turned[:, :PACK]
        gt_slots = gates_turned[:, PACK : 2 * PACK]

        b_window = [sbuf("b_window%d" % t, [P, 2 * N], F32) for t in range(PACK)]
        for t in range(PACK):
            nc.vector.memset(b_window[t][:, N:], 0.0)

        half_gi = sbuf("half_gi", [P, PACK], F32)
        nc.scalar.activation(half_gi[:], gi_slots, ACT.Abs, scale=0.5)
        sign_or_zero = sbuf("sign_or_zero", [P, PACK], F32)
        nc.scalar.activation(sign_or_zero[:], gi_slots, ACT.Sign)
        minus_gi = sbuf("minus_gi", [P, PACK], F32)
        nc.scalar.activation(minus_gi[:], half_gi[:], ACT.Copy, scale=-2.0)
        sign = sbuf("sign", [P, PACK], F32)
        nc.scalar.activation(sign[:], sign_or_zero[:], ACT.Sign, bias=zero_half[:, 1:2])
        signed_gt = sbuf("signed_gt", [P, PACK], F32)
        for t in range(PACK):
            nc.scalar.activation(signed_gt[:, t : t + 1], gt_slots[:, t : t + 1], ACT.Copy, scale=sign[:, t : t + 1])

        def pick_scales(name, offsets):
            picked = sbuf(name, [P, S], U8)
            nc.vector.tensor_copy(picked[:], scale_table[:].indirect(offsets[:]))
            return picked

        def deal_scales(name, picked):
            dealt = sbuf(name, [P, S], U8)
            nc.vector.tensor_copy(
                dealt[:].bitcast(I32).rearrange("p (t g) -> p t g", t=PACK),
                picked[:].bitcast(I32).rearrange("p (g t) -> p t g", t=PACK),
            )
            return dealt

        def pick_words(name, offsets):
            dealt = sbuf(name, [P, S], U32)
            nc.vector.tensor_copy(
                dealt[:].rearrange("p (t g q) -> p g t q", t=PACK, q=RUN),
                word_table[:].bitcast(U32).indirect(offsets[:]),
            )
            return dealt

        xb_picked = pick_scales("xb_picked", two_list)
        xa_picked = pick_scales("xa_picked", offs_list)
        xb_scales = deal_scales("xb_scales", xb_picked)
        xa_scales = deal_scales("xa_scales", xa_picked)
        wb_words = sbuf("wb_words", [P, N], U32)
        wb_scales = sbuf("wb_scales", [P, N], U8)
        wb_woven = sbuf("wb_woven", [P, PACK * N], BF16)
        weave(nc.scalar.copy, wb_woven[:, : PACK * N // 2], wb_raw[:, :, : N // 2])
        weave(nc.vector.tensor_copy, wb_woven[:, PACK * N // 2 :], wb_raw[:, :, N // 2 :])
        nc.vector.quantize_mx(wb_words[:].bitcast(FP8X4), wb_scales[:], wb_woven[:])
        xb_words = pick_words("xb_words", two_list)
        b_acc = [
            product(t, xb_words[:, block(t)], xb_scales[:, block(t)], wb_words[:], wb_scales[:]) for t in range(PACK)
        ]

        xa_words = pick_words("xa_words", offs_list)
        wa_woven = sbuf("wa_woven", [P, PACK * H], BF16)
        weave(nc.vector.tensor_copy, wa_woven[:], wa_raw[:])
        wa_words = sbuf("wa_words", [P, H], U32)
        wa_scales = sbuf("wa_scales", [P, H], U8)

        b_plain = [sbuf("b_plain%d" % t, [P, N], F32) for t in range(PACK)]
        a_window = [sbuf("a_window%d" % t, [P, H], F32) for t in range(PACK)]
        gate = [sbuf("gate%d" % t, [P, W], F32) for t in range(PACK)]
        z_slots = sbuf("z_slots", [P, PACK, H], BF16)

        def b_out(t):
            nc.scalar.copy(b_window[t][:, :N], b_acc[t][:])
            if t < SCALAR_COPIES:
                nc.scalar.copy(b_plain[t][:], b_acc[t][:])
            else:
                nc.sync.dma_start(b_plain[t][:], b_window[t][:, :N])

        z2_sum = [bank(SUM_BANK + f) for f in range(PACK)]

        def b_differences(t):
            d3 = sbuf("d3_%d" % t, [P, N], F32)
            nc.vector.tensor_tensor(d3[:], b_window[t][:].indirect(n3_list[:]), b_plain[t][:], ALU.subtract)
            d4 = sbuf("d4_%d" % t, [P, N], F32)
            nc.vector.tensor_tensor(d4[:], b_window[t][:].indirect(n4_list[:]), b_plain[t][:], ALU.subtract)
            return d3, d4

        def z2_add(t, d3, d4):
            r3 = sbuf("r3_%d" % t, [P, N], F32)
            nc.scalar.activation(r3[:], d3[:], ACT.Relu, scale=minus_gi[:, t : t + 1])
            r4 = sbuf("r4_%d" % t, [P, N], F32)
            nc.scalar.activation(r4[:], d4[:], ACT.Relu, scale=half_gi[:, t : t + 1])
            for f in range(PACK):
                transposed_sum(z2_sum[f][:, block(t)], r3[:, block(f)], r4[:, block(f)])

        z2_turned = [sbuf("z2_turned%d" % f, [P, S], BF16) for f in range(PACK)]
        z2_woven = sbuf("z2_woven", [P, PACK * N], BF16)

        def z2_round(f):
            nc.scalar.copy(
                z2_turned[f][:].rearrange("c (v p e) -> c v p e", v=2, e=2),
                z2_sum[f][:].rearrange("c (v e p) -> c v p e", v=2, e=2),
            )

        def z2_turn_back(h):
            pairs_back = bank(SUM_BANK + h)
            for s in range(2):
                pairs = z2_turned[2 * h + s][:].bitcast(F32)
                for v in range(2):
                    nc.tensor.transpose(pairs_back[:, block(2 * s + v)], pairs[:, block(v)], ident[:])
            return pairs_back

        def z2_weave(h, pairs_back):
            half = slice(h * PACK * N // 2, (h + 1) * PACK * N // 2)
            nc.scalar.copy(
                z2_woven[:, half].bitcast(F32).rearrange("p (s c v) -> p s c v", s=2, v=2),
                pairs_back[:].rearrange("p (s v c) -> p s c v", s=2, v=2),
            )

        def a_out(t):
            nc.scalar.copy(a_window[t][:], a_acc[t][:])

        def a_gate(t):
            nc.scalar.activation(gate[t][:], a_window[t][:].indirect(n2_list[:]), ACT.Sigmoid)

        def a_pick(t):
            pa = sbuf("pa%d" % t, [P, W], F32)
            nc.vector.tensor_copy(pa[:], a_window[t][:].indirect(n1_list[:]))
            return pa

        def a_fold(t, pa):
            nc.vector.tensor_tensor(a_window[t][:].indirect(n2_list[:]), pa[:], gate[t][:], ALU.mult)

        def z_round(t, first, end):
            nc.scalar.activation(
                z_slots[:, t, :].rearrange("p (u m) -> p m u", u=PACK)[:, :, first:end],
                a_window[t][:].rearrange("p (m u) -> p m u", u=PACK)[:, :, first:end],
                ACT.Copy, scale=signed_gt[:, t : t + 1],
            )

        differences = []
        for t in range(PACK):
            b_out(t)
            differences.append(b_differences(t))
            if t == 0:
                nc.vector.quantize_mx(wa_words[:].bitcast(FP8X4), wa_scales[:], wa_woven[:])
        a_acc = [
            product(t, xa_words[:, block(t)], xa_scales[:, block(t)], wa_words[:], wa_scales[:]) for t in range(PACK)
        ]
        pa_slots = []
        for t in range(PACK):
            z2_add(t, *differences[t])
            a_out(t)
            pa_slots.append(a_pick(t))
            if t > 0:
                a_gate(t - 1)
                a_fold(t - 1, pa_slots[t - 1])
        for f in range(PACK):
            z2_round(f)
        z2_pairs = [z2_turn_back(h) for h in range(2)]
        a_gate(LAST)
        a_fold(LAST, pa_slots[LAST])
        z_round(0, 0, PACK)
        z_round(1, 0, PACK)
        for h in range(2):
            z2_weave(h, z2_pairs[h])
        z_round(2, 0, PACK)
        z_round(LAST, 0, 1)
        z_round(LAST, 1, PACK)
        z2_words = sbuf("z2_words", [P, N], U32)
        z2_scales = sbuf("z2_scales", [P, N], U8)
        nc.vector.quantize_mx(z2_words[:].bitcast(FP8X4), z2_scales[:], z2_woven[:])

        z_words = [sbuf("z_words%d" % u, [P, P], U32) for u in range(PACK)]
        z_scales = [sbuf("z_scales%d" % u, [P, P], U8) for u in range(PACK)]
        z_woven = [sbuf("z_woven%d" % u, [P, PACK * P], BF16) for u in range(PACK)]
        out_rows = out.rearrange("(m u) n -> m u n", u=PACK)
        ds2 = [sbuf("ds2_%d" % u, [P, 2 * N], F32) for u in range(PACK)]
        minus_half_cv = [sbuf("minus_half_cv%d" % u, [P, N], F32) for u in range(PACK)]
        rl = [sbuf("rl%d" % u, [P, N], F32) for u in range(PACK)]

        def z_weave(u, copy):
            weave(copy, z_woven[u][:], z_slots[:, :, block(u)])

        def moment(u):
            nc.vector.quantize_mx(z_words[u][:].bitcast(FP8X4), z_scales[u][:], z_woven[u][:])
            return product(u, z_words[u][:], z_scales[u][:], z2_words[:], z2_scales[:])

        def rl_out(u):
            nc.scalar.activation(rl[u][:], cv_acc[u][:], ACT.Relu, scale=0.0625)

        def half_out(u):
            nc.scalar.activation(minus_half_cv[u][:], cv_acc[u][:], ACT.Copy, scale=-0.5 * 0.0625)

        def send(u):
            nc.vector.tensor_copy(ds2[u][:].indirect(n5_list[:]), rl[u][:])

        def finish_by_transposes(u):
            turned_acc = bank(TURNED_BANK)
            for c in range(PACK):
                transposed_sum(turned_acc[:, block(c)], minus_half_cv[u][:, block(c)], ds2[u][:, block(c)])
            turned = sbuf("turned%d" % u, [P, N], F32)
            nc.scalar.copy(turned[:], turned_acc[:])
            back_acc = bank(BACK_BANK)
            for c in range(PACK):
                nc.tensor.transpose(back_acc[:, block(c)], turned[:, block(c)], ident[:])
            result = sbuf("result%d" % u, [P, N], F32)
            nc.scalar.copy(result[:], back_acc[:])
            nc.scalar.dma_start(out_rows[:, u, :], result[:])

        z_weave(0, nc.vector.tensor_copy)
        cv_acc = [moment(0)]
        z_weave(1, nc.vector.tensor_copy)
        z_weave(2, nc.vector.tensor_copy)
        cv_acc.extend([moment(1), moment(2)])
        rl_out(0)
        send(0)
        z_weave(LAST, nc.scalar.copy)
        cv_acc.append(moment(LAST))
        rl_out(1)
        rl_out(2)
        for u in range(LAST):
            half_out(u)
        rl_out(LAST)
        half_out(LAST)
        for u in range(1, PACK):
            send(u)
            finish_by_transposes(u - 1)
        for h in range(2):
            half = slice(h * N // 2, (h + 1) * N // 2)
            result = sbuf("result_last%d" % h, [P, N // 2], F32)
            nc.vector.tensor_tensor(result[:], ds2[LAST][:, half], minus_half_cv[LAST][:, half], ALU.add)
            nc.sync.dma_start(out_rows[:, LAST, half], result[:])
